import numpy as np
CORES = [21,109,149,237,277,365,405,493,150,406]
N = 10
TK = 128
EPS = 0.01
GRP = [[0,1,2,3,4,7],[5,6,8,9]]
def setup_inputs(rng):
    return {"x": rng.standard_normal((N, 128, TK), dtype=np.float32) * (0.5 + np.abs(rng.standard_normal((1, 1, TK), dtype=np.float32))) + rng.standard_normal((1, 1, TK), dtype=np.float32)}
def setup_inputs_big(rng):
    d = setup_inputs(rng)
    for k in ("x",): d[k] = (d[k].astype(np.float32) * 1024.0).astype(d[k].dtype)
    return d
def setup_inputs_small(rng):
    d = setup_inputs(rng)
    for k in ("x",): d[k] = (d[k].astype(np.float32) * (1 / 1024.0)).astype(d[k].dtype)
    return d
def setup_inputs_apart(rng):
    d = setup_inputs(rng)
    f = (10.0 ** rng.permutation(np.linspace(-1.5, 1.5, N))).astype(np.float32).reshape(N, 1, 1)
    for k in ("x",): d[k] = (d[k].astype(np.float32) * f).astype(d[k].dtype)
    return d
def setup_inputs_mixed(rng):
    d = setup_inputs(rng)
    f = (10.0 ** rng.uniform(-3, 3, (1, 1, TK))).astype(np.float32); shape = rng.integers(3, size=(1, 1, TK))
    for k in ("x",):
        x = d[k].astype(np.float32)
        m = x.mean(axis=(0, 1), keepdims=True); level = m + np.sign(x - m) * np.abs(x - m).mean(axis=(0, 1), keepdims=True) * rng.uniform(0.9, 1.1, x.shape).astype(np.float32)
        other = x * np.where(rng.random(x.shape) < 0.5, 0.1, 1.0).astype(np.float32)
        d[k] = (np.where(shape == 1, level, np.where(shape == 2, other, x)) * f).astype(d[k].dtype)
    return d
def setup_inputs_offset(rng):
    d = setup_inputs(rng)
    x = d["x"]; spread = x.std(axis=(0, 1), keepdims=True)
    d["x"] = (x + spread * rng.uniform(16, 48, (1, 1, TK)) * rng.choice([-1.0, 1.0], (1, 1, TK))).astype(np.float32)
    return d
def reference(x):
    X = x.astype(np.float64); y = np.zeros_like(X)
    for m in GRP:
        Z = X[m]; D = 128 * len(m)
        Z = Z - Z.sum(axis=(0, 1)) / D
        y[m] = Z / np.sqrt((Z ** 2).sum(axis=(0, 1)) / D + EPS)
    return {"y": y.astype(np.float32)}

@@ -1,0 +1,206 @@
+import math
+from concourse.bass import DstId, RemoteDMATransfer
+from concourse.mybir import AluOpType, AxisListType, ActivationFunctionType
+
+NSIM = 512
+EPS = 0.01
+NE = 8
+OWN = 2
+FIRST = 4
+
+SCRATCH = {
+    "xs": ("sbuf", [128, 128], "float32"),
+    "ident": ("sbuf", [128, 128], "float32"),
+    "zt": ("sbuf", [128, 128], "float32"),
+    "land": ("sbuf", [128, 16], "float32"),
+    "col": ("sbuf", [128, 16], "float32"),
+    "pt": ("psum", [128, 128], "float32"),
+}
+SEMAPHORES = ["ld", "ones", "idn", "eps", "t", "ns", "b", "st", "arr", "sent", "mu", "b2", "dev", "sd", "z", "v", "r", "a",
+              "bb", "yt", "yp", "y", "out"]
+
+_CACHE = {}
+
+
+def _same_chip(topo, a, b):
+    return topo.host(a) == topo.host(b) and topo.chip(a) == topo.chip(b)
+
+
+def _links(topo, a, b):
+    x = 0.0 if topo.die(a) == topo.die(b) else 0.1
+    if _same_chip(topo, a, b):
+        return x
+    if topo.rack(topo.host(a)) == topo.rack(topo.host(b)):
+        return x + (1 if (topo.mates(a, b) or topo.same_plane(a, b)) else 2)
+    return x + (1 if topo.chip(a) == topo.chip(b) else 3)
+
+
+def _subsets(G, k):
+    if k == 1:
+        return [(a,) for a in G]
+    return [(G[i], G[j]) for i in range(len(G)) for j in range(i + 1, len(G))]
+
+
+def _plan(cores, groups, topo):
+    ranks = set(cores)
+    free = [c for c in range(NSIM) if c not in ranks and any(_same_chip(topo, c, r) for r in cores)]
+    first = {c: [] for c in cores}
+    direct = {c: [] for c in cores}
+    relay = {}
+    col = {c: FIRST for c in cores}
+    nin = {c: 0 for c in cores}
+    for grp in groups:
+        G = [cores[r] for r in grp]
+        open_ = set((s, d) for s in G for d in G if s != d and not topo.may_write(s, d))
+        while open_:
+            best = None
+            for k in (2, 1):
+                for D in _subsets(G, k):
+                    cand = [s for s in G if all((s, d) in open_ for d in D)]
+                    if not cand:
+                        continue
+                    for h in free:
+                        if not all(topo.may_write(h, d) for d in D):
+                            continue
+                        S = [s for s in cand if topo.may_write(s, h)]
+                        if not S:
+                            continue
+                        cost = sum(_links(topo, s, h) for s in S) + sum(_links(topo, h, d) for d in D)
+                        key = (len(S) * len(D), len(D), -cost, -h)
+                        if best is None or key > best[0]:
+                            best = (key, h, S, D)
+            h, S, D = best[1], best[2], best[3]
+            free.remove(h)
+            for j, s in enumerate(S):
+                first[s].append((h, 2 * j))
+            outs = []
+            for d in D:
+                outs.append((d, col[d]))
+                col[d] += 2 * len(S)
+                nin[d] += 1
+            relay[h] = (len(S), outs)
+            nin[h] = len(S)
+            for s in S:
+                for d in D:
+                    open_.discard((s, d))
+        for s in G:
+            for d in G:
+                if s != d and topo.may_write(s, d):
+                    direct[s].append((d, col[d]))
+                    col[d] += 2
+                    nin[d] += 1
+    return {"first": first, "direct": direct, "relay": relay, "nin": nin}
+
+
+def _engines(topo, core, dsts, n):
+    m = -1
+    for d in dsts:
+        m &= topo.mask(core, d)
+    out, k, b = 0, 0, 0
+    while k < n:
+        if (m >> b) & 1:
+            out |= 1 << b
+            k += 1
+        b += 1
+    return out
+
+
+def _send(g, core, T, topo, c0, width, outs):
+    ids = []
+    for d, c in outs:
+        rid, pid = topo.addr(d, core)
+        ids.append(DstId(rid=rid, pnc=pid))
+    g.remote_dma_fused([RemoteDMATransfer(dst_ids=ids, dma_engine_mask=_engines(topo, core, [d for d, c in outs], NE),
+                                          remote_sem=T.sem.arr, srcs=[T.land[:, c0:c0 + width]],
+                                          dsts=[T.land[:, c:c + width] for d, c in outs], alu_op=0)],
+                       local_sem=T.sem.sent)
+    return NE
+
+
+def rank_program(g, core, T, topo):
+    cores = list(T.cores)
+    if not any(_same_chip(topo, core, r) for r in cores):
+        return
+    if "p" not in _CACHE:
+        _CACHE["p"] = _plan(cores, T.tables["GRP"], topo)
+    P = _CACHE["p"]
+    sem = T.sem
+    rank = T.rank_of(core)
+
+    if rank is None:
+        if core not in P["relay"]:
+            return
+        k, outs = P["relay"][core]
+        g.wait_ge(sem.arr, NE * k)
+        n = _send(g, core, T, topo, 0, 2 * k, outs)
+        g.wait_ge(sem.sent, n)
+        return
+
+    R = [len(grp) for grp in T.tables["GRP"] if rank in grp][0]
+    D = 128 * R
+    A, F = AluOpType, ActivationFunctionType
+    V, S, PE, Q = g.vector, g.scalar, g.tensor, g.sync
+    C = T.col
+    means = T.land[:, OWN:2 * R + 2:2]
+    quads = T.land[:, 1:2 * R + 2:2]
+
+    Q.dma_start(T.xs[:], T.x[:]).then_inc(sem.ld, 16)
+    V.memset(T.ident[:], 1.0).then_inc(sem.ones, 1)
+    V.memset(T.land[:, 0:2], EPS).then_inc(sem.eps, 1)
+    g.wait_ge(sem.ones, 1)
+    g.affine_select(T.ident[:], T.ident[:], [[-1, 128]], A.is_equal, 0.0, 0, 1).then_inc(sem.idn, 1)
+
+    PE.wait_ge(sem.ld, 16)
+    PE.wait_ge(sem.idn, 1)
+    PE.transpose(T.pt[:], T.xs[:], T.ident[:]).then_inc(sem.t, 1)
+    V.wait_ge(sem.t, 1)
+    V.tensor_reduce(C[:, 0:1], T.pt[:], AxisListType.X, A.add, negate=True).then_inc(sem.ns, 1)
+    V.wait_ge(sem.ns, 1)
+    V.tensor_scalar(C[:, 1:2], C[:, 0:1], 1.0 / (128.0 * math.sqrt(D)), None, A.mult).then_inc(sem.b, 1)
+    V.tensor_scalar(T.land[:, OWN:OWN + 1], C[:, 0:1], -1.0 / (128.0 * R), None, A.mult).then_inc(sem.st, 1)
+    S.wait_ge(sem.b, 1)
+    S.activation(T.zt[:], T.pt[:], F.Square, bias=C[:, 1:2], scale=1.0 / math.sqrt(D),
+                 accum_out=T.land[:, OWN + 1:OWN + 2]).then_inc(sem.st, 1)
+
+    g.wait_ge(sem.st, 2)
+    n = 0
+    if P["first"][core]:
+        n += _send(g, core, T, topo, OWN, 2, P["first"][core])
+    if P["direct"][core]:
+        n += _send(g, core, T, topo, OWN, 2, P["direct"][core])
+
+    V.wait_ge(sem.arr, NE * P["nin"][core])
+    V.wait_ge(sem.st, 2)
+    V.wait_ge(sem.eps, 1)
+    V.tensor_reduce(C[:, 2:3], means, AxisListType.X, A.add, negate=True).then_inc(sem.mu, 1)
+    V.tensor_reduce(C[:, 3:4], quads, AxisListType.X, A.add).then_inc(sem.b2, 1)
+    S.wait_ge(sem.mu, 1)
+    S.activation(C[:, 8:8 + R], means, F.Square, bias=C[:, 2:3], scale=float(R),
+                 accum_out=C[:, 4:5]).then_inc(sem.dev, 1)
+    S.wait_ge(sem.dev, 1)
+    S.wait_ge(sem.b2, 1)
+    S.activation(C[:, 5:6], C[:, 4:5], F.Sqrt, bias=C[:, 3:4], scale=1.0 / R).then_inc(sem.sd, 1)
+    V.wait_ge(sem.mu, 1)
+    V.tensor_scalar(T.zt[:], T.pt[:], C[:, 2:3], None, A.add).then_inc(sem.z, 1)
+    V.wait_ge(sem.dev, 1)
+    V.wait_ge(sem.b2, 1)
+    V.tensor_scalar(C[:, 6:7], C[:, 4:5], 1.0 / R, C[:, 3:4], A.mult, A.add).then_inc(sem.v, 1)
+    V.wait_ge(sem.sd, 1)
+    V.reciprocal(C[:, 7:8], C[:, 5:6]).then_inc(sem.r, 1)
+    V.wait_ge(sem.r, 1)
+    V.wait_ge(sem.v, 1)
+    V.tensor_scalar(C[:, 14:15], C[:, 7:8], C[:, 6:7], C[:, 7:8], A.mult, A.mult).then_inc(sem.a, 1)
+    V.wait_ge(sem.a, 1)
+    V.tensor_scalar(C[:, 15:16], C[:, 14:15], -0.5, 1.5, A.mult, A.add).then_inc(sem.bb, 1)
+    V.wait_ge(sem.bb, 1)
+    V.wait_ge(sem.z, 1)
+    V.tensor_scalar(T.zt[:], T.zt[:], C[:, 7:8], C[:, 15:16], A.mult, A.mult).then_inc(sem.yt, 1)
+
+    PE.wait_ge(sem.yt, 1)
+    PE.transpose(T.pt[:], T.zt[:], T.ident[:]).then_inc(sem.yp, 1)
+    V.wait_ge(sem.yp, 1)
+    V.tensor_copy(T.xs[:], T.pt[:]).then_inc(sem.y, 1)
+    Q.wait_ge(sem.y, 1)
+    Q.dma_start(T.y[:], T.xs[:]).then_inc(sem.out, 16)
+    Q.wait_ge(sem.out, 16)
+    g.wait_ge(sem.sent, n)

@@ -4,7 +4,8 @@ from concourse.mybir import AluOpType, AxisListType, ActivationFunctionType
 
 NSIM = 512
 EPS = 0.01
-NE = 8
+NE_S = 8
+NE_H = 8
 OWN = 2
 FIRST = 4
 
@@ -13,11 +14,11 @@ SCRATCH = {
     "ident": ("sbuf", [128, 128], "float32"),
     "zt": ("sbuf", [128, 128], "float32"),
     "land": ("sbuf", [128, 16], "float32"),
-    "col": ("sbuf", [128, 16], "float32"),
+    "col": ("sbuf", [128, 24], "float32"),
     "pt": ("psum", [128, 128], "float32"),
 }
-SEMAPHORES = ["ld", "ones", "idn", "eps", "t", "ns", "b", "st", "arr", "sent", "mu", "b2", "dev", "sd", "z", "v", "r", "a",
-              "bb", "yt", "yp", "y", "out"]
+SEMAPHORES = ["ld", "ones", "idn", "eps", "t", "ns", "b", "st", "arr", "sent", "sg", "rho", "r2", "mu", "b1", "b2", "dev",
+              "sd", "z", "v", "r", "a", "bb", "yt", "yp", "y", "out"]
 
 _CACHE = {}
 
@@ -48,7 +49,7 @@ def _plan(cores, groups, topo):
     direct = {c: [] for c in cores}
     relay = {}
     col = {c: FIRST for c in cores}
-    nin = {c: 0 for c in cores}
+    inc = {c: 0 for c in cores}
     for grp in groups:
         G = [cores[r] for r in grp]
         open_ = set((s, d) for s in G for d in G if s != d and not topo.may_write(s, d))
@@ -77,9 +78,9 @@ def _plan(cores, groups, topo):
             for d in D:
                 outs.append((d, col[d]))
                 col[d] += 2 * len(S)
-                nin[d] += 1
+                inc[d] += NE_H
             relay[h] = (len(S), outs)
-            nin[h] = len(S)
+            inc[h] = NE_S * len(S)
             for s in S:
                 for d in D:
                     open_.discard((s, d))
@@ -88,8 +89,8 @@ def _plan(cores, groups, topo):
                 if s != d and topo.may_write(s, d):
                     direct[s].append((d, col[d]))
                     col[d] += 2
-                    nin[d] += 1
-    return {"first": first, "direct": direct, "relay": relay, "nin": nin}
+                    inc[d] += NE_S
+    return {"first": first, "direct": direct, "relay": relay, "inc": inc}
 
 
 def _engines(topo, core, dsts, n):
@@ -105,16 +106,16 @@ def _engines(topo, core, dsts, n):
     return out
 
 
-def _send(g, core, T, topo, c0, width, outs):
+def _send(g, core, T, topo, c0, width, outs, ne):
     ids = []
     for d, c in outs:
         rid, pid = topo.addr(d, core)
         ids.append(DstId(rid=rid, pnc=pid))
-    g.remote_dma_fused([RemoteDMATransfer(dst_ids=ids, dma_engine_mask=_engines(topo, core, [d for d, c in outs], NE),
+    g.remote_dma_fused([RemoteDMATransfer(dst_ids=ids, dma_engine_mask=_engines(topo, core, [d for d, c in outs], ne),
                                           remote_sem=T.sem.arr, srcs=[T.land[:, c0:c0 + width]],
                                           dsts=[T.land[:, c:c + width] for d, c in outs], alu_op=0)],
                        local_sem=T.sem.sent)
-    return NE
+    return ne
 
 
 def rank_program(g, core, T, topo):
@@ -131,8 +132,8 @@ def rank_program(g, core, T, topo):
         if core not in P["relay"]:
             return
         k, outs = P["relay"][core]
-        g.wait_ge(sem.arr, NE * k)
-        n = _send(g, core, T, topo, 0, 2 * k, outs)
+        g.wait_ge(sem.arr, P["inc"][core])
+        n = _send(g, core, T, topo, 0, 2 * k, outs, NE_H)
         g.wait_ge(sem.sent, n)
         return
 
@@ -165,26 +166,37 @@ def rank_program(g, core, T, topo):
     g.wait_ge(sem.st, 2)
     n = 0
     if P["first"][core]:
-        n += _send(g, core, T, topo, OWN, 2, P["first"][core])
+        n += _send(g, core, T, topo, OWN, 2, P["first"][core], NE_S)
     if P["direct"][core]:
-        n += _send(g, core, T, topo, OWN, 2, P["direct"][core])
+        n += _send(g, core, T, topo, OWN, 2, P["direct"][core], NE_S)
 
-    V.wait_ge(sem.arr, NE * P["nin"][core])
+    S.wait_ge(sem.st, 2)
+    S.activation(C[:, 16:17], T.land[:, OWN + 1:OWN + 2], F.Sqrt, bias=EPS, scale=1.0).then_inc(sem.sg, 1)
+    V.wait_ge(sem.sg, 1)
+    V.reciprocal(C[:, 17:18], C[:, 16:17]).then_inc(sem.rho, 1)
+    V.wait_ge(sem.rho, 1)
+    V.tensor_scalar(C[:, 18:19], C[:, 17:18], C[:, 17:18], None, A.mult).then_inc(sem.r2, 1)
+    V.tensor_scalar(C[:, 19:20], C[:, 17:18], C[:, 17:18], 1.0 / R, A.mult, A.mult).then_inc(sem.r2, 1)
+
+    V.wait_ge(sem.arr, P["inc"][core])
     V.wait_ge(sem.st, 2)
     V.wait_ge(sem.eps, 1)
+    V.wait_ge(sem.r2, 2)
     V.tensor_reduce(C[:, 2:3], means, AxisListType.X, A.add, negate=True).then_inc(sem.mu, 1)
-    V.tensor_reduce(C[:, 3:4], quads, AxisListType.X, A.add).then_inc(sem.b2, 1)
+    V.tensor_reduce(C[:, 3:4], quads, AxisListType.X, A.add).then_inc(sem.b1, 1)
+    V.wait_ge(sem.b1, 1)
+    V.tensor_scalar(C[:, 20:21], C[:, 3:4], C[:, 18:19], None, A.mult).then_inc(sem.b2, 1)
     S.wait_ge(sem.mu, 1)
     S.activation(C[:, 8:8 + R], means, F.Square, bias=C[:, 2:3], scale=float(R),
                  accum_out=C[:, 4:5]).then_inc(sem.dev, 1)
     S.wait_ge(sem.dev, 1)
     S.wait_ge(sem.b2, 1)
-    S.activation(C[:, 5:6], C[:, 4:5], F.Sqrt, bias=C[:, 3:4], scale=1.0 / R).then_inc(sem.sd, 1)
+    S.activation(C[:, 5:6], C[:, 4:5], F.Sqrt, bias=C[:, 20:21], scale=C[:, 19:20]).then_inc(sem.sd, 1)
     V.wait_ge(sem.mu, 1)
-    V.tensor_scalar(T.zt[:], T.pt[:], C[:, 2:3], None, A.add).then_inc(sem.z, 1)
+    V.tensor_scalar(T.zt[:], T.pt[:], C[:, 2:3], C[:, 17:18], A.add, A.mult).then_inc(sem.z, 1)
     V.wait_ge(sem.dev, 1)
     V.wait_ge(sem.b2, 1)
-    V.tensor_scalar(C[:, 6:7], C[:, 4:5], 1.0 / R, C[:, 3:4], A.mult, A.add).then_inc(sem.v, 1)
+    V.tensor_scalar(C[:, 6:7], C[:, 4:5], C[:, 19:20], C[:, 20:21], A.mult, A.add).then_inc(sem.v, 1)
     V.wait_ge(sem.sd, 1)
     V.reciprocal(C[:, 7:8], C[:, 5:6]).then_inc(sem.r, 1)
     V.wait_ge(sem.r, 1)

@@ -6,19 +6,24 @@ NSIM = 512
 EPS = 0.01
 NE_S = 8
 NE_H = 8
+NE_R = 4
 OWN = 2
 FIRST = 4
 
 SCRATCH = {
     "xs": ("sbuf", [128, 128], "float32"),
     "ident": ("sbuf", [128, 128], "float32"),
+    "e2": ("sbuf", [128, 64], "float32"),
+    "dg": ("sbuf", [128, 64], "float32"),
     "zt": ("sbuf", [128, 128], "float32"),
     "land": ("sbuf", [128, 16], "float32"),
-    "col": ("sbuf", [128, 24], "float32"),
-    "pt": ("psum", [128, 128], "float32"),
+    "col": ("sbuf", [128, 48], "float32"),
+    "pt": ("psum", [128, 512], "float32"),
+    "pa": ("psum", [128, 512], "float32"),
+    "pb": ("psum", [128, 512], "float32"),
 }
-SEMAPHORES = ["ld", "ones", "idn", "eps", "t", "ns", "b", "st", "arr", "sent", "sg", "rho", "r2", "mu", "b1", "b2", "dev",
-              "sd", "z", "v", "r", "a", "bb", "yt", "yp", "y", "out"]
+SEMAPHORES = ["lda", "ldb", "ones", "idn", "eps", "t", "ns", "b", "st", "arr", "rl", "sent", "sg", "rho", "r2", "e1", "mu", "b2",
+              "dev", "sd", "z", "v", "r", "hs", "hr", "nf", "dgs", "ya", "yb", "ca", "cb", "oa", "ob"]
 
 _CACHE = {}
 
@@ -47,12 +52,23 @@ def _plan(cores, groups, topo):
     free = [c for c in range(NSIM) if c not in ranks and any(_same_chip(topo, c, r) for r in cores)]
     first = {c: [] for c in cores}
     direct = {c: [] for c in cores}
+    handed = {c: [] for c in cores}
+    hand = {c: [] for c in cores}
     relay = {}
     col = {c: FIRST for c in cores}
     inc = {c: 0 for c in cores}
+    inc2 = {c: 0 for c in cores}
     for grp in groups:
         G = [cores[r] for r in grp]
         open_ = set((s, d) for s in G for d in G if s != d and not topo.may_write(s, d))
+        via = {}
+        for s, d in sorted(open_):
+            cand = [r for r in G if r != s and r != d and topo.may_write(s, r) and topo.may_write(r, d)
+                    and len([1 for p in via if via[p] == r]) < NE_S // NE_R]
+            if cand:
+                via[s, d] = min(cand, key=lambda r: (_links(topo, s, r) + _links(topo, r, d), r))
+        for p in via:
+            open_.discard(p)
         while open_:
             best = None
             for k in (2, 1):
@@ -84,37 +100,51 @@ def _plan(cores, groups, topo):
             for s in S:
                 for d in D:
                     open_.discard((s, d))
+        where = {}
         for s in G:
             for d in G:
                 if s != d and topo.may_write(s, d):
-                    direct[s].append((d, col[d]))
+                    where[s, d] = col[d]
+                    if any(p[0] == s and via[p] == d for p in via):
+                        handed[s].append((d, col[d]))
+                        inc2[d] += NE_S
+                    else:
+                        direct[s].append((d, col[d]))
+                        inc[d] += NE_S
                     col[d] += 2
-                    inc[d] += NE_S
-    return {"first": first, "direct": direct, "relay": relay, "inc": inc}
+        for s, d in sorted(via):
+            hand[via[s, d]].append((where[s, via[s, d]], d, col[d]))
+            col[d] += 2
+            inc[d] += NE_R
+    return {"first": first, "direct": direct, "handed": handed, "hand": hand, "relay": relay, "inc": inc, "inc2": inc2}
 
 
-def _engines(topo, core, dsts, n):
+def _engines(topo, core, dsts, n, skip=0):
     m = -1
     for d in dsts:
         m &= topo.mask(core, d)
     out, k, b = 0, 0, 0
-    while k < n:
+    while k < skip + n:
         if (m >> b) & 1:
-            out |= 1 << b
+            if k >= skip:
+                out |= 1 << b
             k += 1
         b += 1
     return out
 
 
-def _send(g, core, T, topo, c0, width, outs, ne):
+def _transfer(core, T, topo, c0, width, outs, ne, rsem, skip=0):
     ids = []
     for d, c in outs:
         rid, pid = topo.addr(d, core)
         ids.append(DstId(rid=rid, pnc=pid))
-    g.remote_dma_fused([RemoteDMATransfer(dst_ids=ids, dma_engine_mask=_engines(topo, core, [d for d, c in outs], ne),
-                                          remote_sem=T.sem.arr, srcs=[T.land[:, c0:c0 + width]],
-                                          dsts=[T.land[:, c:c + width] for d, c in outs], alu_op=0)],
-                       local_sem=T.sem.sent)
+    return RemoteDMATransfer(dst_ids=ids, dma_engine_mask=_engines(topo, core, [d for d, c in outs], ne, skip),
+                             remote_sem=rsem, srcs=[T.land[:, c0:c0 + width]],
+                             dsts=[T.land[:, c:c + width] for d, c in outs], alu_op=0)
+
+
+def _send(g, core, T, topo, c0, width, outs, ne, rsem):
+    g.remote_dma_fused([_transfer(core, T, topo, c0, width, outs, ne, rsem)], local_sem=T.sem.sent)
     return ne
 
 
@@ -133,7 +163,7 @@ def rank_program(g, core, T, topo):
             return
         k, outs = P["relay"][core]
         g.wait_ge(sem.arr, P["inc"][core])
-        n = _send(g, core, T, topo, 0, 2 * k, outs, NE_H)
+        n = _send(g, core, T, topo, 0, 2 * k, outs, NE_H, sem.arr)
         g.wait_ge(sem.sent, n)
         return
 
@@ -142,77 +172,106 @@ def rank_program(g, core, T, topo):
     A, F = AluOpType, ActivationFunctionType
     V, S, PE, Q = g.vector, g.scalar, g.tensor, g.sync
     C = T.col
+    xT = T.pt[:, 0:128]
     means = T.land[:, OWN:2 * R + 2:2]
     quads = T.land[:, 1:2 * R + 2:2]
 
-    Q.dma_start(T.xs[:], T.x[:]).then_inc(sem.ld, 16)
+    Q.dma_start(T.xs[0:64, :], T.x[0:64, :]).then_inc(sem.lda, 16)
+    S.dma_start(T.xs[64:128, :], T.x[64:128, :]).then_inc(sem.ldb, 16)
     V.memset(T.ident[:], 1.0).then_inc(sem.ones, 1)
     V.memset(T.land[:, 0:2], EPS).then_inc(sem.eps, 1)
     g.wait_ge(sem.ones, 1)
     g.affine_select(T.ident[:], T.ident[:], [[-1, 128]], A.is_equal, 0.0, 0, 1).then_inc(sem.idn, 1)
 
-    PE.wait_ge(sem.ld, 16)
     PE.wait_ge(sem.idn, 1)
-    PE.transpose(T.pt[:], T.xs[:], T.ident[:]).then_inc(sem.t, 1)
-    V.wait_ge(sem.t, 1)
-    V.tensor_reduce(C[:, 0:1], T.pt[:], AxisListType.X, A.add, negate=True).then_inc(sem.ns, 1)
+    PE.wait_ge(sem.lda, 16)
+    PE.transpose(T.pt[:, 0:64], T.xs[0:64, :], T.ident[0:64, 0:64]).then_inc(sem.t, 1)
+    PE.wait_ge(sem.ldb, 16)
+    PE.wait_ge(sem.t, 1)
+    PE.transpose(T.pt[:, 64:128], T.xs[64:128, :], T.ident[64:128, 64:128]).then_inc(sem.t, 1)
+    V.wait_ge(sem.t, 2)
+    V.tensor_reduce(C[:, 0:1], xT, AxisListType.X, A.add, negate=True).then_inc(sem.ns, 1)
     V.wait_ge(sem.ns, 1)
     V.tensor_scalar(C[:, 1:2], C[:, 0:1], 1.0 / (128.0 * math.sqrt(D)), None, A.mult).then_inc(sem.b, 1)
     V.tensor_scalar(T.land[:, OWN:OWN + 1], C[:, 0:1], -1.0 / (128.0 * R), None, A.mult).then_inc(sem.st, 1)
     S.wait_ge(sem.b, 1)
-    S.activation(T.zt[:], T.pt[:], F.Square, bias=C[:, 1:2], scale=1.0 / math.sqrt(D),
+    S.activation(T.zt[:], xT, F.Square, bias=C[:, 1:2], scale=1.0 / math.sqrt(D),
                  accum_out=T.land[:, OWN + 1:OWN + 2]).then_inc(sem.st, 1)
 
     g.wait_ge(sem.st, 2)
     n = 0
     if P["first"][core]:
-        n += _send(g, core, T, topo, OWN, 2, P["first"][core], NE_S)
+        n += _send(g, core, T, topo, OWN, 2, P["first"][core], NE_S, sem.arr)
+    if P["handed"][core]:
+        n += _send(g, core, T, topo, OWN, 2, P["handed"][core], NE_S, sem.rl)
     if P["direct"][core]:
-        n += _send(g, core, T, topo, OWN, 2, P["direct"][core], NE_S)
+        n += _send(g, core, T, topo, OWN, 2, P["direct"][core], NE_S, sem.arr)
+    if P["hand"][core]:
+        g.wait_ge(sem.rl, P["inc2"][core])
+        g.remote_dma_fused([_transfer(core, T, topo, c0, 2, [(d, c)], NE_R, sem.arr, NE_R * i)
+                            for i, (c0, d, c) in enumerate(P["hand"][core])], local_sem=sem.sent)
+        n += NE_R * len(P["hand"][core])
 
     S.wait_ge(sem.st, 2)
     S.activation(C[:, 16:17], T.land[:, OWN + 1:OWN + 2], F.Sqrt, bias=EPS, scale=1.0).then_inc(sem.sg, 1)
+    V.wait_ge(sem.idn, 1)
+    V.tensor_tensor(T.e2[:], T.ident[:, 0:64], T.ident[:, 64:128], A.add).then_inc(sem.e1, 1)
     V.wait_ge(sem.sg, 1)
     V.reciprocal(C[:, 17:18], C[:, 16:17]).then_inc(sem.rho, 1)
     V.wait_ge(sem.rho, 1)
     V.tensor_scalar(C[:, 18:19], C[:, 17:18], C[:, 17:18], None, A.mult).then_inc(sem.r2, 1)
     V.tensor_scalar(C[:, 19:20], C[:, 17:18], C[:, 17:18], 1.0 / R, A.mult, A.mult).then_inc(sem.r2, 1)
+    V.tensor_scalar(C[:, 21:22], C[:, 17:18], 0.5, None, A.mult).then_inc(sem.r2, 1)
 
-    V.wait_ge(sem.arr, P["inc"][core])
+    V.wait_ge(sem.r2, 3)
+    V.wait_ge(sem.e1, 1)
     V.wait_ge(sem.st, 2)
-    V.wait_ge(sem.eps, 1)
-    V.wait_ge(sem.r2, 2)
+    if P["inc2"][core]:
+        V.wait_ge(sem.rl, P["inc2"][core])
+    V.wait_ge(sem.arr, P["inc"][core])
     V.tensor_reduce(C[:, 2:3], means, AxisListType.X, A.add, negate=True).then_inc(sem.mu, 1)
-    V.tensor_reduce(C[:, 3:4], quads, AxisListType.X, A.add).then_inc(sem.b1, 1)
-    V.wait_ge(sem.b1, 1)
-    V.tensor_scalar(C[:, 20:21], C[:, 3:4], C[:, 18:19], None, A.mult).then_inc(sem.b2, 1)
+    S.wait_ge(sem.r2, 3)
+    S.wait_ge(sem.eps, 1)
+    if P["inc2"][core]:
+        S.wait_ge(sem.rl, P["inc2"][core])
+    S.wait_ge(sem.arr, P["inc"][core])
+    S.activation(C[:, 32:33 + R], quads, F.Identity, scale=C[:, 18:19],
+                 accum_out=C[:, 20:21]).then_inc(sem.b2, 1)
     S.wait_ge(sem.mu, 1)
-    S.activation(C[:, 8:8 + R], means, F.Square, bias=C[:, 2:3], scale=float(R),
+    S.activation(C[:, 24:24 + R], means, F.Square, bias=C[:, 2:3], scale=float(R),
                  accum_out=C[:, 4:5]).then_inc(sem.dev, 1)
     S.wait_ge(sem.dev, 1)
     S.wait_ge(sem.b2, 1)
     S.activation(C[:, 5:6], C[:, 4:5], F.Sqrt, bias=C[:, 20:21], scale=C[:, 19:20]).then_inc(sem.sd, 1)
-    V.wait_ge(sem.mu, 1)
-    V.tensor_scalar(T.zt[:], T.pt[:], C[:, 2:3], C[:, 17:18], A.add, A.mult).then_inc(sem.z, 1)
     V.wait_ge(sem.dev, 1)
     V.wait_ge(sem.b2, 1)
     V.tensor_scalar(C[:, 6:7], C[:, 4:5], C[:, 19:20], C[:, 20:21], A.mult, A.add).then_inc(sem.v, 1)
     V.wait_ge(sem.sd, 1)
-    V.reciprocal(C[:, 7:8], C[:, 5:6]).then_inc(sem.r, 1)
-    V.wait_ge(sem.r, 1)
     V.wait_ge(sem.v, 1)
-    V.tensor_scalar(C[:, 14:15], C[:, 7:8], C[:, 6:7], C[:, 7:8], A.mult, A.mult).then_inc(sem.a, 1)
-    V.wait_ge(sem.a, 1)
-    V.tensor_scalar(C[:, 15:16], C[:, 14:15], -0.5, 1.5, A.mult, A.add).then_inc(sem.bb, 1)
-    V.wait_ge(sem.bb, 1)
-    V.wait_ge(sem.z, 1)
-    V.tensor_scalar(T.zt[:], T.zt[:], C[:, 7:8], C[:, 15:16], A.mult, A.mult).then_inc(sem.yt, 1)
+    V.reciprocal(C[:, 10:12], C[:, 5:7]).then_inc(sem.r, 1)
+    S.wait_ge(sem.sd, 1)
+    S.activation(C[:, 9:10], C[:, 5:6], F.Square, scale=math.sqrt(0.5)).then_inc(sem.hs, 1)
+    S.wait_ge(sem.hs, 1)
+    S.activation(C[:, 12:13], C[:, 9:10], F.Identity, scale=C[:, 17:18]).then_inc(sem.hr, 1)
+    S.activation(T.zt[:], xT, F.Identity, bias=C[:, 2:3], scale=1.0).then_inc(sem.z, 1)
+    V.wait_ge(sem.r, 1)
+    V.wait_ge(sem.hr, 1)
+    V.tensor_scalar(C[:, 13:14], C[:, 12:13], C[:, 11:12], C[:, 21:22], A.mult, A.add).then_inc(sem.nf, 1)
+    V.wait_ge(sem.nf, 1)
+    V.tensor_scalar(T.dg[:], T.e2[:], C[:, 10:11], C[:, 13:14], A.mult, A.mult).then_inc(sem.dgs, 1)
 
-    PE.wait_ge(sem.yt, 1)
-    PE.transpose(T.pt[:], T.zt[:], T.ident[:]).then_inc(sem.yp, 1)
-    V.wait_ge(sem.yp, 1)
-    V.tensor_copy(T.xs[:], T.pt[:]).then_inc(sem.y, 1)
-    Q.wait_ge(sem.y, 1)
-    Q.dma_start(T.y[:], T.xs[:]).then_inc(sem.out, 16)
-    Q.wait_ge(sem.out, 16)
+    PE.wait_ge(sem.z, 1)
+    PE.wait_ge(sem.dgs, 1)
+    PE.matmul(T.pa[:, 0:64], T.zt[0:64, :], T.dg[0:64, :], True, True).then_inc(sem.ya, 1)
+    PE.matmul(T.pb[:, 0:64], T.zt[64:128, :], T.dg[64:128, :], True, True).then_inc(sem.yb, 1)
+    V.wait_ge(sem.ya, 1)
+    V.tensor_copy(T.xs[:, 0:64], T.pa[:, 0:64]).then_inc(sem.ca, 1)
+    Q.wait_ge(sem.ca, 1)
+    Q.dma_start(T.y[:, 0:64], T.xs[:, 0:64]).then_inc(sem.oa, 16)
+    V.wait_ge(sem.yb, 1)
+    V.tensor_copy(T.xs[:, 64:128], T.pb[:, 0:64]).then_inc(sem.cb, 1)
+    S.wait_ge(sem.cb, 1)
+    S.dma_start(T.y[:, 64:128], T.xs[:, 64:128]).then_inc(sem.ob, 16)
+    Q.wait_ge(sem.oa, 16)
+    S.wait_ge(sem.ob, 16)
     g.wait_ge(sem.sent, n)

@@ -7,23 +7,25 @@ EPS = 0.01
 NE_S = 8
 NE_H = 8
 NE_R = 4
-OWN = 2
-FIRST = 4
+W = 4
+OWN = 4
+FIRST = 8
 
 SCRATCH = {
-    "xs": ("sbuf", [128, 128], "float32"),
-    "ident": ("sbuf", [128, 128], "float32"),
+    "xs": ("sbuf", [128, 256], "float32"),
+    "ys": ("sbuf", [128, 128], "float32"),
     "e2": ("sbuf", [128, 64], "float32"),
     "dg": ("sbuf", [128, 64], "float32"),
     "zt": ("sbuf", [128, 128], "float32"),
-    "land": ("sbuf", [128, 16], "float32"),
-    "col": ("sbuf", [128, 48], "float32"),
+    "land": ("sbuf", [128, 32], "float32"),
+    "col": ("sbuf", [128, 80], "float32"),
     "pt": ("psum", [128, 512], "float32"),
+    "pu": ("psum", [128, 512], "float32"),
     "pa": ("psum", [128, 512], "float32"),
     "pb": ("psum", [128, 512], "float32"),
 }
-SEMAPHORES = ["lda", "ldb", "ones", "idn", "eps", "t", "ns", "b", "st", "arr", "rl", "sent", "sg", "rho", "r2", "e1", "mu", "b2",
-              "dev", "sd", "z", "v", "r", "hs", "hr", "nf", "dgs", "ya", "yb", "ca", "cb", "oa", "ob"]
+SEMAPHORES = ["lda", "ldb", "ones", "idn", "idm", "eps", "ta", "tb", "na", "nb", "st", "arr", "rl", "sent", "q0", "sg", "rho", "r2",
+              "mu", "b2", "dev", "sd", "z", "v", "r", "hs", "hr", "nf", "dgs", "ya", "yb", "ca", "cb", "oa", "ob"]
 
 _CACHE = {}
 
@@ -89,11 +91,11 @@ def _plan(cores, groups, topo):
             h, S, D = best[1], best[2], best[3]
             free.remove(h)
             for j, s in enumerate(S):
-                first[s].append((h, 2 * j))
+                first[s].append((h, W * j))
             outs = []
             for d in D:
                 outs.append((d, col[d]))
-                col[d] += 2 * len(S)
+                col[d] += W * len(S)
                 inc[d] += NE_H
             relay[h] = (len(S), outs)
             inc[h] = NE_S * len(S)
@@ -111,10 +113,10 @@ def _plan(cores, groups, topo):
                     else:
                         direct[s].append((d, col[d]))
                         inc[d] += NE_S
-                    col[d] += 2
+                    col[d] += W
         for s, d in sorted(via):
             hand[via[s, d]].append((where[s, via[s, d]], d, col[d]))
-            col[d] += 2
+            col[d] += W
             inc[d] += NE_R
     return {"first": first, "direct": direct, "handed": handed, "hand": hand, "relay": relay, "inc": inc, "inc2": inc2}
 
@@ -163,82 +165,86 @@ def rank_program(g, core, T, topo):
             return
         k, outs = P["relay"][core]
         g.wait_ge(sem.arr, P["inc"][core])
-        n = _send(g, core, T, topo, 0, 2 * k, outs, NE_H, sem.arr)
+        n = _send(g, core, T, topo, 0, W * k, outs, NE_H, sem.arr)
         g.wait_ge(sem.sent, n)
         return
 
     R = [len(grp) for grp in T.tables["GRP"] if rank in grp][0]
     D = 128 * R
+    NP = 2 * R
+    KAP = 1.0 / (64.0 * math.sqrt(D))
     A, F = AluOpType, ActivationFunctionType
     V, S, PE, Q = g.vector, g.scalar, g.tensor, g.sync
-    C = T.col
-    xT = T.pt[:, 0:128]
-    means = T.land[:, OWN:2 * R + 2:2]
-    quads = T.land[:, 1:2 * R + 2:2]
+    C, L = T.col, T.land
+    ev, od = T.pt[:, 0:64], T.pu[:, 0:64]
+    means = L[:, OWN:OWN + 4 * R:2]
+    quads = L[:, OWN - 1:OWN + 4 * R:2]
 
-    Q.dma_start(T.xs[0:64, :], T.x[0:64, :]).then_inc(sem.lda, 16)
-    S.dma_start(T.xs[64:128, :], T.x[64:128, :]).then_inc(sem.ldb, 16)
-    V.memset(T.ident[:], 1.0).then_inc(sem.ones, 1)
-    V.memset(T.land[:, 0:2], EPS).then_inc(sem.eps, 1)
+    Q.dma_start(T.xs[0:32, :], T.x[0:64, :]).then_inc(sem.lda, 16)
+    S.dma_start(T.xs[32:64, :], T.x[64:128, :]).then_inc(sem.ldb, 16)
+    V.memset(T.e2[:], KAP).then_inc(sem.ones, 1)
+    V.memset(L[:, 0:4], EPS).then_inc(sem.eps, 1)
     g.wait_ge(sem.ones, 1)
-    g.affine_select(T.ident[:], T.ident[:], [[-1, 128]], A.is_equal, 0.0, 0, 1).then_inc(sem.idn, 1)
+    g.affine_select(T.e2[0:64, :], T.e2[0:64, :], [[-1, 64]], A.is_equal, 0.0, 0, 1).then_inc(sem.idn, 1)
+    g.affine_select(T.e2[64:128, :], T.e2[64:128, :], [[-1, 64]], A.is_equal, 0.0, 0, 1).then_inc(sem.idm, 1)
 
     PE.wait_ge(sem.idn, 1)
     PE.wait_ge(sem.lda, 16)
-    PE.transpose(T.pt[:, 0:64], T.xs[0:64, :], T.ident[0:64, 0:64]).then_inc(sem.t, 1)
     PE.wait_ge(sem.ldb, 16)
-    PE.wait_ge(sem.t, 1)
-    PE.transpose(T.pt[:, 64:128], T.xs[64:128, :], T.ident[64:128, 64:128]).then_inc(sem.t, 1)
-    V.wait_ge(sem.t, 2)
-    V.tensor_reduce(C[:, 0:1], xT, AxisListType.X, A.add, negate=True).then_inc(sem.ns, 1)
-    V.wait_ge(sem.ns, 1)
-    V.tensor_scalar(C[:, 1:2], C[:, 0:1], 1.0 / (128.0 * math.sqrt(D)), None, A.mult).then_inc(sem.b, 1)
-    V.tensor_scalar(T.land[:, OWN:OWN + 1], C[:, 0:1], -1.0 / (128.0 * R), None, A.mult).then_inc(sem.st, 1)
-    S.wait_ge(sem.b, 1)
-    S.activation(T.zt[:], xT, F.Square, bias=C[:, 1:2], scale=1.0 / math.sqrt(D),
-                 accum_out=T.land[:, OWN + 1:OWN + 2]).then_inc(sem.st, 1)
+    PE.matmul(ev, T.xs[0:64, 0:128], T.e2[0:64, :], True, True).then_inc(sem.ta, 1)
+    PE.matmul(od, T.xs[0:64, 128:256], T.e2[0:64, :], True, True).then_inc(sem.tb, 1)
+    V.wait_ge(sem.ta, 1)
+    V.tensor_reduce(L[:, OWN:OWN + 1], ev, AxisListType.X, A.add, negate=True).then_inc(sem.na, 1)
+    S.wait_ge(sem.na, 1)
+    S.activation(T.zt[:, 0:64], ev, F.Square, bias=L[:, OWN:OWN + 1], scale=64.0,
+                 accum_out=L[:, OWN + 1:OWN + 2]).then_inc(sem.st, 1)
+    V.wait_ge(sem.tb, 1)
+    V.tensor_reduce(L[:, OWN + 2:OWN + 3], od, AxisListType.X, A.add, negate=True).then_inc(sem.nb, 1)
+    S.wait_ge(sem.nb, 1)
+    S.activation(T.zt[:, 64:128], od, F.Square, bias=L[:, OWN + 2:OWN + 3], scale=64.0,
+                 accum_out=L[:, OWN + 3:OWN + 4]).then_inc(sem.st, 1)
 
     g.wait_ge(sem.st, 2)
     n = 0
     if P["first"][core]:
-        n += _send(g, core, T, topo, OWN, 2, P["first"][core], NE_S, sem.arr)
+        n += _send(g, core, T, topo, OWN, W, P["first"][core], NE_S, sem.arr)
     if P["handed"][core]:
-        n += _send(g, core, T, topo, OWN, 2, P["handed"][core], NE_S, sem.rl)
+        n += _send(g, core, T, topo, OWN, W, P["handed"][core], NE_S, sem.rl)
     if P["direct"][core]:
-        n += _send(g, core, T, topo, OWN, 2, P["direct"][core], NE_S, sem.arr)
+        n += _send(g, core, T, topo, OWN, W, P["direct"][core], NE_S, sem.arr)
     if P["hand"][core]:
         g.wait_ge(sem.rl, P["inc2"][core])
-        g.remote_dma_fused([_transfer(core, T, topo, c0, 2, [(d, c)], NE_R, sem.arr, NE_R * i)
+        g.remote_dma_fused([_transfer(core, T, topo, c0, W, [(d, c)], NE_R, sem.arr, NE_R * i)
                             for i, (c0, d, c) in enumerate(P["hand"][core])], local_sem=sem.sent)
         n += NE_R * len(P["hand"][core])
 
-    S.wait_ge(sem.st, 2)
-    S.activation(C[:, 16:17], T.land[:, OWN + 1:OWN + 2], F.Sqrt, bias=EPS, scale=1.0).then_inc(sem.sg, 1)
-    V.wait_ge(sem.idn, 1)
-    V.tensor_tensor(T.e2[:], T.ident[:, 0:64], T.ident[:, 64:128], A.add).then_inc(sem.e1, 1)
+    V.wait_ge(sem.st, 2)
+    V.tensor_scalar(C[:, 15:16], L[:, OWN + 1:OWN + 2], L[:, OWN + 3:OWN + 4], EPS, A.add, A.add).then_inc(sem.q0, 1)
+    S.wait_ge(sem.q0, 1)
+    S.activation(C[:, 16:17], C[:, 15:16], F.Sqrt).then_inc(sem.sg, 1)
     V.wait_ge(sem.sg, 1)
     V.reciprocal(C[:, 17:18], C[:, 16:17]).then_inc(sem.rho, 1)
     V.wait_ge(sem.rho, 1)
     V.tensor_scalar(C[:, 18:19], C[:, 17:18], C[:, 17:18], None, A.mult).then_inc(sem.r2, 1)
-    V.tensor_scalar(C[:, 19:20], C[:, 17:18], C[:, 17:18], 1.0 / R, A.mult, A.mult).then_inc(sem.r2, 1)
-    V.tensor_scalar(C[:, 21:22], C[:, 17:18], 0.5, None, A.mult).then_inc(sem.r2, 1)
+    V.tensor_scalar(C[:, 19:20], C[:, 17:18], C[:, 17:18], 64.0 / (NP * NP), A.mult, A.mult).then_inc(sem.r2, 1)
+    V.tensor_scalar(C[:, 21:22], C[:, 17:18], -2048.0, None, A.mult).then_inc(sem.r2, 1)
+    V.tensor_scalar(C[:, 22:23], C[:, 17:18], -1.0, None, A.mult).then_inc(sem.r2, 1)
 
-    V.wait_ge(sem.r2, 3)
-    V.wait_ge(sem.e1, 1)
-    V.wait_ge(sem.st, 2)
+    V.wait_ge(sem.r2, 4)
+    V.wait_ge(sem.idm, 1)
     if P["inc2"][core]:
         V.wait_ge(sem.rl, P["inc2"][core])
     V.wait_ge(sem.arr, P["inc"][core])
     V.tensor_reduce(C[:, 2:3], means, AxisListType.X, A.add, negate=True).then_inc(sem.mu, 1)
-    S.wait_ge(sem.r2, 3)
+    S.wait_ge(sem.r2, 4)
     S.wait_ge(sem.eps, 1)
     if P["inc2"][core]:
         S.wait_ge(sem.rl, P["inc2"][core])
     S.wait_ge(sem.arr, P["inc"][core])
-    S.activation(C[:, 32:33 + R], quads, F.Identity, scale=C[:, 18:19],
+    S.activation(C[:, 32:33 + NP], quads, F.Identity, scale=C[:, 18:19],
                  accum_out=C[:, 20:21]).then_inc(sem.b2, 1)
     S.wait_ge(sem.mu, 1)
-    S.activation(C[:, 24:24 + R], means, F.Square, bias=C[:, 2:3], scale=float(R),
+    S.activation(C[:, 48:48 + NP], means, F.Square, bias=C[:, 2:3], scale=float(NP),
                  accum_out=C[:, 4:5]).then_inc(sem.dev, 1)
     S.wait_ge(sem.dev, 1)
     S.wait_ge(sem.b2, 1)
@@ -250,28 +256,29 @@ def rank_program(g, core, T, topo):
     V.wait_ge(sem.v, 1)
     V.reciprocal(C[:, 10:12], C[:, 5:7]).then_inc(sem.r, 1)
     S.wait_ge(sem.sd, 1)
-    S.activation(C[:, 9:10], C[:, 5:6], F.Square, scale=math.sqrt(0.5)).then_inc(sem.hs, 1)
+    S.activation(C[:, 9:10], C[:, 5:6], F.Square, scale=math.sqrt(2048.0)).then_inc(sem.hs, 1)
     S.wait_ge(sem.hs, 1)
-    S.activation(C[:, 12:13], C[:, 9:10], F.Identity, scale=C[:, 17:18]).then_inc(sem.hr, 1)
-    S.activation(T.zt[:], xT, F.Identity, bias=C[:, 2:3], scale=1.0).then_inc(sem.z, 1)
+    S.activation(C[:, 12:13], C[:, 9:10], F.Identity, scale=C[:, 22:23]).then_inc(sem.hr, 1)
+    S.activation(T.zt[:, 0:128:2], ev, F.Identity, bias=C[:, 2:3], scale=-float(D)).then_inc(sem.z, 1)
+    S.activation(T.zt[:, 1:128:2], od, F.Identity, bias=C[:, 2:3], scale=-float(D)).then_inc(sem.z, 1)
     V.wait_ge(sem.r, 1)
     V.wait_ge(sem.hr, 1)
     V.tensor_scalar(C[:, 13:14], C[:, 12:13], C[:, 11:12], C[:, 21:22], A.mult, A.add).then_inc(sem.nf, 1)
     V.wait_ge(sem.nf, 1)
     V.tensor_scalar(T.dg[:], T.e2[:], C[:, 10:11], C[:, 13:14], A.mult, A.mult).then_inc(sem.dgs, 1)
 
-    PE.wait_ge(sem.z, 1)
+    PE.wait_ge(sem.z, 2)
     PE.wait_ge(sem.dgs, 1)
     PE.matmul(T.pa[:, 0:64], T.zt[0:64, :], T.dg[0:64, :], True, True).then_inc(sem.ya, 1)
     PE.matmul(T.pb[:, 0:64], T.zt[64:128, :], T.dg[64:128, :], True, True).then_inc(sem.yb, 1)
     V.wait_ge(sem.ya, 1)
-    V.tensor_copy(T.xs[:, 0:64], T.pa[:, 0:64]).then_inc(sem.ca, 1)
+    V.tensor_copy(T.ys[:, 0:64], T.pa[:, 0:64]).then_inc(sem.ca, 1)
     Q.wait_ge(sem.ca, 1)
-    Q.dma_start(T.y[:, 0:64], T.xs[:, 0:64]).then_inc(sem.oa, 16)
+    Q.dma_start(T.y[:, 0:64], T.ys[:, 0:64]).then_inc(sem.oa, 16)
     V.wait_ge(sem.yb, 1)
-    V.tensor_copy(T.xs[:, 64:128], T.pb[:, 0:64]).then_inc(sem.cb, 1)
+    V.tensor_copy(T.ys[:, 64:128], T.pb[:, 0:64]).then_inc(sem.cb, 1)
     S.wait_ge(sem.cb, 1)
-    S.dma_start(T.y[:, 64:128], T.xs[:, 64:128]).then_inc(sem.ob, 16)
+    S.dma_start(T.y[:, 64:128], T.ys[:, 64:128]).then_inc(sem.ob, 16)
     Q.wait_ge(sem.oa, 16)
     S.wait_ge(sem.ob, 16)
     g.wait_ge(sem.sent, n)

import math
from concourse.bass import DstId, RemoteDMATransfer
from concourse.mybir import AluOpType, AxisListType, ActivationFunctionType

NSIM = 512
EPS = 0.01
NE_S = 8
NE_H = 8
NE_R = 4
W = 4
OWN = 4
FIRST = 8

SCRATCH = {
    "xs": ("sbuf", [128, 256], "float32"),
    "ys": ("sbuf", [128, 128], "float32"),
    "e2": ("sbuf", [128, 64], "float32"),
    "dg": ("sbuf", [128, 64], "float32"),
    "zt": ("sbuf", [128, 128], "float32"),
    "land": ("sbuf", [128, 32], "float32"),
    "col": ("sbuf", [128, 80], "float32"),
    "pt": ("psum", [128, 512], "float32"),
    "pu": ("psum", [128, 512], "float32"),
    "pa": ("psum", [128, 512], "float32"),
    "pb": ("psum", [128, 512], "float32"),
}
SEMAPHORES = ["lda", "ldb", "ones", "idn", "idm", "eps", "ta", "tb", "na", "nb", "st", "arr", "rl", "sent", "q0", "sg", "rho", "r2",
              "mu", "b2", "dev", "sd", "z", "v", "r", "hs", "hr", "nf", "dgs", "ya", "yb", "ca", "cb", "oa", "ob"]

_CACHE = {}


def _same_chip(topo, a, b):
    return topo.host(a) == topo.host(b) and topo.chip(a) == topo.chip(b)


def _links(topo, a, b):
    x = 0.0 if topo.die(a) == topo.die(b) else 0.1
    if _same_chip(topo, a, b):
        return x
    if topo.rack(topo.host(a)) == topo.rack(topo.host(b)):
        return x + (1 if (topo.mates(a, b) or topo.same_plane(a, b)) else 2)
    return x + (1 if topo.chip(a) == topo.chip(b) else 3)


def _subsets(G, k):
    if k == 1:
        return [(a,) for a in G]
    return [(G[i], G[j]) for i in range(len(G)) for j in range(i + 1, len(G))]


def _plan(cores, groups, topo):
    ranks = set(cores)
    free = [c for c in range(NSIM) if c not in ranks and any(_same_chip(topo, c, r) for r in cores)]
    first = {c: [] for c in cores}
    direct = {c: [] for c in cores}
    handed = {c: [] for c in cores}
    hand = {c: [] for c in cores}
    relay = {}
    col = {c: FIRST for c in cores}
    inc = {c: 0 for c in cores}
    inc2 = {c: 0 for c in cores}
    for grp in groups:
        G = [cores[r] for r in grp]
        open_ = set((s, d) for s in G for d in G if s != d and not topo.may_write(s, d))
        via = {}
        for s, d in sorted(open_):
            cand = [r for r in G if r != s and r != d and topo.may_write(s, r) and topo.may_write(r, d)
                    and len([1 for p in via if via[p] == r]) < NE_S // NE_R]
            if cand:
                via[s, d] = min(cand, key=lambda r: (_links(topo, s, r) + _links(topo, r, d), r))
        for p in via:
            open_.discard(p)
        while open_:
            best = None
            for k in (2, 1):
                for D in _subsets(G, k):
                    cand = [s for s in G if all((s, d) in open_ for d in D)]
                    if not cand:
                        continue
                    for h in free:
                        if not all(topo.may_write(h, d) for d in D):
                            continue
                        S = [s for s in cand if topo.may_write(s, h)]
                        if not S:
                            continue
                        cost = sum(_links(topo, s, h) for s in S) + sum(_links(topo, h, d) for d in D)
                        key = (len(S) * len(D), len(D), -cost, -h)
                        if best is None or key > best[0]:
                            best = (key, h, S, D)
            h, S, D = best[1], best[2], best[3]
            free.remove(h)
            for j, s in enumerate(S):
                first[s].append((h, W * j))
            outs = []
            for d in D:
                outs.append((d, col[d]))
                col[d] += W * len(S)
                inc[d] += NE_H
            relay[h] = (len(S), outs)
            inc[h] = NE_S * len(S)
            for s in S:
                for d in D:
                    open_.discard((s, d))
        where = {}
        for s in G:
            for d in G:
                if s != d and topo.may_write(s, d):
                    where[s, d] = col[d]
                    if any(p[0] == s and via[p] == d for p in via):
                        handed[s].append((d, col[d]))
                        inc2[d] += NE_S
                    else:
                        direct[s].append((d, col[d]))
                        inc[d] += NE_S
                    col[d] += W
        for s, d in sorted(via):
            hand[via[s, d]].append((where[s, via[s, d]], d, col[d]))
            col[d] += W
            inc[d] += NE_R
    return {"first": first, "direct": direct, "handed": handed, "hand": hand, "relay": relay, "inc": inc, "inc2": inc2}


def _engines(topo, core, dsts, n, skip=0):
    m = -1
    for d in dsts:
        m &= topo.mask(core, d)
    out, k, b = 0, 0, 0
    while k < skip + n:
        if (m >> b) & 1:
            if k >= skip:
                out |= 1 << b
            k += 1
        b += 1
    return out


def _transfer(core, T, topo, c0, width, outs, ne, rsem, skip=0):
    ids = []
    for d, c in outs:
        rid, pid = topo.addr(d, core)
        ids.append(DstId(rid=rid, pnc=pid))
    return RemoteDMATransfer(dst_ids=ids, dma_engine_mask=_engines(topo, core, [d for d, c in outs], ne, skip),
                             remote_sem=rsem, srcs=[T.land[:, c0:c0 + width]],
                             dsts=[T.land[:, c:c + width] for d, c in outs], alu_op=0)


def _send(g, core, T, topo, c0, width, outs, ne, rsem):
    g.remote_dma_fused([_transfer(core, T, topo, c0, width, outs, ne, rsem)], local_sem=T.sem.sent)
    return ne


def rank_program(g, core, T, topo):
    cores = list(T.cores)
    if not any(_same_chip(topo, core, r) for r in cores):
        return
    if "p" not in _CACHE:
        _CACHE["p"] = _plan(cores, T.tables["GRP"], topo)
    P = _CACHE["p"]
    sem = T.sem
    rank = T.rank_of(core)

    if rank is None:
        if core not in P["relay"]:
            return
        k, outs = P["relay"][core]
        g.wait_ge(sem.arr, P["inc"][core])
        n = _send(g, core, T, topo, 0, W * k, outs, NE_H, sem.arr)
        g.wait_ge(sem.sent, n)
        return

    R = [len(grp) for grp in T.tables["GRP"] if rank in grp][0]
    D = 128 * R
    NP = 2 * R
    KAP = 1.0 / (64.0 * math.sqrt(D))
    A, F = AluOpType, ActivationFunctionType
    V, S, PE, Q = g.vector, g.scalar, g.tensor, g.sync
    C, L = T.col, T.land
    ev, od = T.pt[:, 0:64], T.pu[:, 0:64]
    means = L[:, OWN:OWN + 4 * R:2]
    quads = L[:, OWN - 1:OWN + 4 * R:2]

    Q.dma_start(T.xs[0:32, :], T.x[0:64, :]).then_inc(sem.lda, 16)
    S.dma_start(T.xs[32:64, :], T.x[64:128, :]).then_inc(sem.ldb, 16)
    V.memset(T.e2[:], KAP).then_inc(sem.ones, 1)
    V.memset(L[:, 0:4], EPS).then_inc(sem.eps, 1)
    g.wait_ge(sem.ones, 1)
    g.affine_select(T.e2[0:64, :], T.e2[0:64, :], [[-1, 64]], A.is_equal, 0.0, 0, 1).then_inc(sem.idn, 1)
    g.affine_select(T.e2[64:128, :], T.e2[64:128, :], [[-1, 64]], A.is_equal, 0.0, 0, 1).then_inc(sem.idm, 1)

    PE.wait_ge(sem.idn, 1)
    PE.wait_ge(sem.lda, 16)
    PE.wait_ge(sem.ldb, 16)
    PE.matmul(ev, T.xs[0:64, 0:128], T.e2[0:64, :], True, True).then_inc(sem.ta, 1)
    PE.matmul(od, T.xs[0:64, 128:256], T.e2[0:64, :], True, True).then_inc(sem.tb, 1)
    V.wait_ge(sem.ta, 1)
    V.tensor_reduce(L[:, OWN:OWN + 1], ev, AxisListType.X, A.add, negate=True).then_inc(sem.na, 1)
    S.wait_ge(sem.na, 1)
    S.activation(T.zt[:, 0:64], ev, F.Square, bias=L[:, OWN:OWN + 1], scale=64.0,
                 accum_out=L[:, OWN + 1:OWN + 2]).then_inc(sem.st, 1)
    V.wait_ge(sem.tb, 1)
    V.tensor_reduce(L[:, OWN + 2:OWN + 3], od, AxisListType.X, A.add, negate=True).then_inc(sem.nb, 1)
    S.wait_ge(sem.nb, 1)
    S.activation(T.zt[:, 64:128], od, F.Square, bias=L[:, OWN + 2:OWN + 3], scale=64.0,
                 accum_out=L[:, OWN + 3:OWN + 4]).then_inc(sem.st, 1)

    g.wait_ge(sem.st, 2)
    n = 0
    if P["first"][core]:
        n += _send(g, core, T, topo, OWN, W, P["first"][core], NE_S, sem.arr)
    if P["handed"][core]:
        n += _send(g, core, T, topo, OWN, W, P["handed"][core], NE_S, sem.rl)
    if P["direct"][core]:
        n += _send(g, core, T, topo, OWN, W, P["direct"][core], NE_S, sem.arr)
    if P["hand"][core]:
        g.wait_ge(sem.rl, P["inc2"][core])
        g.remote_dma_fused([_transfer(core, T, topo, c0, W, [(d, c)], NE_R, sem.arr, NE_R * i)
                            for i, (c0, d, c) in enumerate(P["hand"][core])], local_sem=sem.sent)
        n += NE_R * len(P["hand"][core])

    V.wait_ge(sem.st, 2)
    V.tensor_scalar(C[:, 15:16], L[:, OWN + 1:OWN + 2], L[:, OWN + 3:OWN + 4], EPS, A.add, A.add).then_inc(sem.q0, 1)
    S.wait_ge(sem.q0, 1)
    S.activation(C[:, 16:17], C[:, 15:16], F.Sqrt).then_inc(sem.sg, 1)
    V.wait_ge(sem.sg, 1)
    V.reciprocal(C[:, 17:18], C[:, 16:17]).then_inc(sem.rho, 1)
    V.wait_ge(sem.rho, 1)
    V.tensor_scalar(C[:, 18:19], C[:, 17:18], C[:, 17:18], None, A.mult).then_inc(sem.r2, 1)
    V.tensor_scalar(C[:, 19:20], C[:, 17:18], C[:, 17:18], 64.0 / (NP * NP), A.mult, A.mult).then_inc(sem.r2, 1)
    V.tensor_scalar(C[:, 21:22], C[:, 17:18], -2048.0, None, A.mult).then_inc(sem.r2, 1)
    V.tensor_scalar(C[:, 22:23], C[:, 17:18], -1.0, None, A.mult).then_inc(sem.r2, 1)

    V.wait_ge(sem.r2, 4)
    V.wait_ge(sem.idm, 1)
    if P["inc2"][core]:
        V.wait_ge(sem.rl, P["inc2"][core])
    V.wait_ge(sem.arr, P["inc"][core])
    V.tensor_reduce(C[:, 2:3], means, AxisListType.X, A.add, negate=True).then_inc(sem.mu, 1)
    S.wait_ge(sem.r2, 4)
    S.wait_ge(sem.eps, 1)
    if P["inc2"][core]:
        S.wait_ge(sem.rl, P["inc2"][core])
    S.wait_ge(sem.arr, P["inc"][core])
    S.activation(C[:, 32:33 + NP], quads, F.Identity, scale=C[:, 18:19],
                 accum_out=C[:, 20:21]).then_inc(sem.b2, 1)
    S.wait_ge(sem.mu, 1)
    S.activation(C[:, 48:48 + NP], means, F.Square, bias=C[:, 2:3], scale=float(NP),
                 accum_out=C[:, 4:5]).then_inc(sem.dev, 1)
    S.wait_ge(sem.dev, 1)
    S.wait_ge(sem.b2, 1)
    S.activation(C[:, 5:6], C[:, 4:5], F.Sqrt, bias=C[:, 20:21], scale=C[:, 19:20]).then_inc(sem.sd, 1)
    V.wait_ge(sem.dev, 1)
    V.wait_ge(sem.b2, 1)
    V.tensor_scalar(C[:, 6:7], C[:, 4:5], C[:, 19:20], C[:, 20:21], A.mult, A.add).then_inc(sem.v, 1)
    V.wait_ge(sem.sd, 1)
    V.wait_ge(sem.v, 1)
    V.reciprocal(C[:, 10:12], C[:, 5:7]).then_inc(sem.r, 1)
    S.wait_ge(sem.sd, 1)
    S.activation(C[:, 9:10], C[:, 5:6], F.Square, scale=math.sqrt(2048.0)).then_inc(sem.hs, 1)
    S.wait_ge(sem.hs, 1)
    S.activation(C[:, 12:13], C[:, 9:10], F.Identity, scale=C[:, 22:23]).then_inc(sem.hr, 1)
    S.activation(T.zt[:, 0:128:2], ev, F.Identity, bias=C[:, 2:3], scale=-float(D)).then_inc(sem.z, 1)
    S.activation(T.zt[:, 1:128:2], od, F.Identity, bias=C[:, 2:3], scale=-float(D)).then_inc(sem.z, 1)
    V.wait_ge(sem.r, 1)
    V.wait_ge(sem.hr, 1)
    V.tensor_scalar(C[:, 13:14], C[:, 12:13], C[:, 11:12], C[:, 21:22], A.mult, A.add).then_inc(sem.nf, 1)
    V.wait_ge(sem.nf, 1)
    V.tensor_scalar(T.dg[:], T.e2[:], C[:, 10:11], C[:, 13:14], A.mult, A.mult).then_inc(sem.dgs, 1)

    PE.wait_ge(sem.z, 2)
    PE.wait_ge(sem.dgs, 1)
    PE.matmul(T.pa[:, 0:64], T.zt[0:64, :], T.dg[0:64, :], True, True).then_inc(sem.ya, 1)
    PE.matmul(T.pb[:, 0:64], T.zt[64:128, :], T.dg[64:128, :], True, True).then_inc(sem.yb, 1)
    V.wait_ge(sem.ya, 1)
    V.tensor_copy(T.ys[:, 0:64], T.pa[:, 0:64]).then_inc(sem.ca, 1)
    Q.wait_ge(sem.ca, 1)
    Q.dma_start(T.y[:, 0:64], T.ys[:, 0:64]).then_inc(sem.oa, 16)
    V.wait_ge(sem.yb, 1)
    V.tensor_copy(T.ys[:, 64:128], T.pb[:, 0:64]).then_inc(sem.cb, 1)
    S.wait_ge(sem.cb, 1)
    S.dma_start(T.y[:, 64:128], T.ys[:, 64:128]).then_inc(sem.ob, 16)
    Q.wait_ge(sem.oa, 16)
    S.wait_ge(sem.ob, 16)
    g.wait_ge(sem.sent, n)
